import numpy as np
import ml_dtypes


def mxq(x, axis, fmt="e4m3"):
    dtype, down = {"e4m3": (ml_dtypes.float8_e4m3fn, 7), "e5m2": (ml_dtypes.float8_e5m2, 14)}[fmt]
    v = np.moveaxis(np.asarray(x, np.float32).astype(ml_dtypes.bfloat16).astype(np.float64), axis, -1)
    blocks = v.reshape(v.shape[:-1] + (-1, 32))
    amax = np.abs(blocks).max(-1, keepdims=True)
    byte = np.maximum(np.where(amax > 0, np.frexp(amax)[1] - 1 + 127, 0) - down, 1)
    scale = np.exp2(byte - 127.0)
    codes = (blocks / scale).astype(np.float32).astype(dtype).astype(np.float64)
    return np.moveaxis((codes * scale).reshape(v.shape), -1, axis)


WIDE = False


def mx_kscale(k):
    if not WIDE:
        return np.ones(k)
    levels = np.array([10, -10, 5, -5, 0])
    if k % 512:
        return np.exp2(np.random.permutation(np.resize(levels, k // 32))).repeat(32)
    a = np.empty((k // 512, 16))
    for p in range(k // 512):
        a[p, :8] = np.random.permutation(np.resize(levels, 8))
        for g in range(8):
            far = levels[np.abs(levels - a[p, g]) >= 10]
            a[p, g + 8] = far[np.random.randint(len(far))]
    return np.exp2(a.ravel()).repeat(32)


def f64(x):
    return np.asarray(x).astype(np.float64)


def striped(idx):
    return np.tile(idx.reshape(-1, 16).T, (8, 1)).astype(np.uint16)


def unstriped(offs):
    return offs[:16].T.reshape(-1).astype(np.int64)


def pack_weight(w):
    k, n = w.shape
    w = f64(np.asarray(w, np.float32).astype(ml_dtypes.bfloat16)).reshape(k // 32, 32, n)
    amax = np.abs(w).max(1)
    byte = np.clip(np.where(amax > 0, np.frexp(amax)[1] - 1 + 127 - 7, 1), 1, 254)
    scaled = (w * np.exp2(127.0 - byte)[:, None, :]).reshape(k, n).astype(np.float32)
    words = np.ascontiguousarray(scaled.reshape(k // 512, 128, 4, n).transpose(0, 1, 3, 2)).astype(ml_dtypes.float8_e4m3fn).view(np.uint8)
    return words, np.ascontiguousarray(byte.astype(np.uint8).reshape(k // 512, 16, n))


def unpack_weight(words, scales):
    g, p, n, _ = words.shape
    vals = np.ascontiguousarray(words).view(ml_dtypes.float8_e4m3fn).astype(np.float64) * np.repeat(np.exp2(scales.astype(np.float64) - 127.0), 8, axis=1)[..., None]
    return vals.transpose(0, 1, 3, 2).reshape(g * 512, n)


def relu(v):
    return np.maximum(v, 0.0)


K, T, S, D, N, V, W, G = 512, 2048, 512, 2, 128, 256, 2048, 1024


def setup_inputs():
    n = np.random.standard_normal
    s = mx_kscale(K)[:, None]
    packed_xT = pack_weight(n((K, T)) * s)
    packed_eT = pack_weight(n((K, W)) * s)
    packed_dT = pack_weight(n((K, G)) * s)
    return {
        "x_words": packed_xT[0],
        "x_scales": packed_xT[1],
        "e_words": packed_eT[0],
        "e_scales": packed_eT[1],
        "d_words": packed_dT[0],
        "d_scales": packed_dT[1],
        "w1": (n((K, N)) / np.sqrt(K) / s).astype(np.float32),
        "w2": (n((K, N)) / np.sqrt(K) / s).astype(np.float32),
        "w3": (n((K, N)) / np.sqrt(K) / s).astype(np.float32),
        "w4": (n((K, N)) / np.sqrt(K) / s).astype(np.float32),
        "offs": striped(np.random.permutation(T)[:S]),
        "seen": striped(np.random.permutation(W)[:S]),
        "state": striped(np.random.permutation(G)[:V]),
    }


def reference(x_words, x_scales, e_words, e_scales, d_words, d_scales, w1, w2, w3, w4, offs, seen, state):
    d_state = unpack_weight(d_words, d_scales)[:, unstriped(state)]
    e_seen = unpack_weight(e_words, e_scales)[:, unstriped(seen)]
    xq = unpack_weight(x_words, x_scales)[:, unstriped(offs)]
    kq = (np.abs(mxq(f64(w2), 0, "e4m3").T @ e_seen)) * ((mxq(f64(w1), 0, "e4m3").T @ xq))
    y = kq.reshape(len(kq), -1, D).mean(axis=2) + (mxq(f64(w3), 0, "e4m3").T @ d_state)
    gg = relu(y) + np.exp(-1.0 * relu(-1.0 * y))
    return (np.abs(mxq(f64(w4), 0, "e4m3").T @ d_state)) * (gg - 1.0)

@@ -1,0 +1,158 @@
+from contextlib import ExitStack
+
+import concourse.mybir as mybir
+
+K, N, S, V, D = 512, 128, 512, 256, 2
+FLOPS = 2 * K * N * (2 * S + 2 * V)
+
+F32 = mybir.dt.float32
+BF16 = mybir.dt.bfloat16
+I32 = mybir.dt.int32
+U32 = mybir.dt.uint32
+U16 = mybir.dt.uint16
+U8 = mybir.dt.uint8
+FP8X4 = mybir.dt.float8_e4m3fn_x4
+ALU = mybir.AluOpType
+ACT = mybir.ActivationFunctionType
+
+P = 128
+PACK = 4
+HALVES = 2
+VH = V // HALVES
+
+
+def tile_picked_yqmix_mix_p_kernel(
+    tc, x_words, x_scales, e_words, e_scales, d_words, d_scales, w1, w2, w3, w4, offs, seen, state, out
+):
+    nc = tc.nc
+    with ExitStack() as ctx:
+        sb = ctx.enter_context(tc.tile_pool(name="sb", bufs=1))
+        ps = ctx.enter_context(tc.psum_pool(name="ps", bufs=1))
+
+        def load_list(src, name):
+            tile = sb.tile(list(src.shape), U16, name=name)
+            nc.sync.dma_start(tile[:], src)
+            return tile
+
+        def clear_scales(src, name):
+            tile = sb.tile([P, src.shape[2]], U8, name=name, align_bytes=64)
+            nc.vector.memset(tile[:].bitcast(I32), 0)
+            return tile
+
+        def load_scales(tile, src, first):
+            for q in range(4):
+                rows = slice(32 * q + first, 32 * q + first + 4)
+                nc.scalar.dma_start(tile[rows, :].bitcast(I32), src[0, 4 * q : 4 * q + 4, :].bitcast(I32))
+
+        def load_words(src, name):
+            tile = sb.tile([P, src.shape[2]], I32, name=name, align_bytes=64)
+            nc.sync.dma_start(tile[:], src[0].rearrange("p n t -> p (n t)").bitcast(I32))
+            return tile
+
+        def load_weight(src, name):
+            tile = sb.tile([P, PACK, N], F32, name=name, align_bytes=64)
+            nc.sync.dma_start(tile[:], src.rearrange("(p j) n -> p j n", j=PACK))
+            return tile
+
+        def quantize(raw, name):
+            grouped = sb.tile([P, N, PACK], BF16, name=name + "_bf16", align_bytes=64)
+            nc.scalar.copy(grouped[:], raw[:].rearrange("p j n -> p n j"))
+            codes = sb.tile([P, N], U32, name=name + "_codes", align_bytes=64)
+            plane = sb.tile([P, N], U8, name=name + "_plane", align_bytes=64)
+            nc.vector.quantize_mx(
+                out=codes[:].bitcast(FP8X4), scales=plane[:], in_=grouped[:].rearrange("p n j -> p (n j)")
+            )
+            return codes, plane
+
+        def product(acc, weight, words, plane):
+            nc.tensor.matmul_mx(
+                out=acc,
+                lhsT=weight[0][:].bitcast(FP8X4),
+                lhsT_scale=weight[1][:],
+                rhs=words.bitcast(FP8X4),
+                rhs_scale=plane,
+                start=True,
+                stop=True,
+            )
+
+        e_first, x_first, d_first = 0, 4, 8
+        e_plane = clear_scales(e_scales, "e_plane")
+        x_plane = clear_scales(x_scales, "x_plane")
+        d_plane = clear_scales(d_scales, "d_plane")
+        zero = sb.tile([P, 1], F32, name="zero")
+        nc.vector.memset(zero[:], 0.0)
+
+        seen_list = load_list(seen, "seen_list")
+        offs_list = load_list(offs, "offs_list")
+        state_list = load_list(state, "state_list")
+        load_scales(e_plane, e_scales, e_first)
+        load_scales(x_plane, x_scales, x_first)
+        one = sb.tile([P, 1], F32, name="one")
+        nc.scalar.activation(one[:], zero[:], ACT.Exp)
+        load_scales(d_plane, d_scales, d_first)
+        e_table = load_words(e_words, "e_table")
+        w2_raw = load_weight(w2, "w2_raw")
+        x_table = load_words(x_words, "x_table")
+        w1_raw = load_weight(w1, "w1_raw")
+        w3_raw = load_weight(w3, "w3_raw")
+        d_table = load_words(d_words, "d_table")
+        w4_raw = load_weight(w4, "w4_raw")
+
+        e_bytes = sb.tile([P, S], U8, name="e_bytes", align_bytes=64)
+        e_codes = sb.tile([P, S], U32, name="e_codes", align_bytes=64)
+        x_bytes = sb.tile([P, S], U8, name="x_bytes", align_bytes=64)
+        x_codes = sb.tile([P, S], U32, name="x_codes", align_bytes=64)
+        d_bytes = sb.tile([P, V], U8, name="d_bytes", align_bytes=64)
+        d_codes = sb.tile([P, V], U32, name="d_codes", align_bytes=64)
+
+        nc.vector.tensor_copy(e_bytes[:], e_plane[:].indirect(seen_list[:]))
+        nc.vector.tensor_copy(e_codes[:], e_table[:].bitcast(U32).indirect(seen_list[:]))
+        nc.vector.tensor_copy(x_bytes[:], x_plane[:].indirect(offs_list[:]))
+        q2 = quantize(w2_raw, "w2")
+        nc.vector.tensor_copy(d_bytes[:], d_plane[:].indirect(state_list[:]))
+        nc.vector.tensor_copy(x_codes[:], x_table[:].bitcast(U32).indirect(offs_list[:]))
+
+        mix_acc = ps.tile([P, S], F32, name="mix_acc")
+        product(mix_acc[:], q2, e_codes[:], e_bytes[e_first:P, :])
+        mix = sb.tile([P, D, V], F32, name="mix")
+        nc.scalar.activation(mix[:], mix_acc[:].rearrange("p (v d) -> p d v", d=D), ACT.Abs, scale=1.0 / D)
+
+        q1 = quantize(w1_raw, "w1")
+        val_acc = ps.tile([P, S], F32, name="val_acc")
+        product(val_acc[:], q1, x_codes[:], x_bytes[x_first:P, :])
+        q3 = quantize(w3_raw, "w3")
+
+        cols = [slice(h * VH, (h + 1) * VH) for h in range(HALVES)]
+        for h in range(HALVES):
+            part = state_list[:, h * VH // 16 : (h + 1) * VH // 16]
+            nc.vector.tensor_copy(d_codes[:, cols[h]], d_table[:].bitcast(U32).indirect(part))
+        bias_acc = [ps.tile([P, VH], F32, name="bias_acc%d" % h) for h in range(HALVES)]
+        for h in range(HALVES):
+            product(bias_acc[h][:], q3, d_codes[:, cols[h]], d_bytes[d_first:P, cols[h]])
+
+        kq = sb.tile([P, D, V], F32, name="kq")
+        nc.vector.tensor_tensor(kq[:], val_acc[:].rearrange("p (v d) -> p d v", d=D), mix[:], ALU.mult)
+        mean = sb.tile([P, V], F32, name="mean")
+        nc.vector.tensor_tensor(mean[:], kq[:, 0, :], kq[:, 1, :], ALU.add)
+
+        q4 = quantize(w4_raw, "w4")
+        gate_acc = ps.tile([P, V], F32, name="gate_acc")
+        product(gate_acc[:], q4, d_codes[:], d_bytes[d_first:P, :])
+        gate = sb.tile([P, V], F32, name="gate")
+        nc.scalar.activation(gate[:], gate_acc[:], ACT.Abs)
+
+        def halves(name):
+            return [sb.tile([P, VH], F32, name="%s%d" % (name, h)) for h in range(HALVES)]
+
+        y, low, ex, elu, res = halves("y"), halves("low"), halves("ex"), halves("elu"), halves("res")
+        for h in range(HALVES):
+            nc.vector.tensor_tensor(y[h][:], bias_acc[h][:], mean[:, cols[h]], ALU.add)
+        for h in range(HALVES):
+            nc.vector.tensor_scalar(low[h][:], y[h][:], 0.0, None, ALU.min)
+        for h in range(HALVES):
+            nc.scalar.activation(ex[h][:], low[h][:], ACT.Exp)
+        for h in range(HALVES):
+            nc.vector.scalar_tensor_tensor(elu[h][:], ex[h][:], one[:], y[h][:], ALU.subtract, ALU.max)
+        for h in range(HALVES):
+            nc.vector.tensor_tensor(res[h][:], elu[h][:], gate[:, cols[h]], ALU.mult)
+            nc.sync.dma_start(out[:, cols[h]], res[h][:])

@@ -39,10 +39,10 @@ def tile_picked_yqmix_mix_p_kernel(
             nc.vector.memset(tile[:].bitcast(I32), 0)
             return tile
 
-        def load_scales(tile, src, first):
+        def load_scales(tile, src, first, queues):
             for q in range(4):
                 rows = slice(32 * q + first, 32 * q + first + 4)
-                nc.scalar.dma_start(tile[rows, :].bitcast(I32), src[0, 4 * q : 4 * q + 4, :].bitcast(I32))
+                queues[q].dma_start(tile[rows, :].bitcast(I32), src[0, 4 * q : 4 * q + 4, :].bitcast(I32))
 
         def load_words(src, name):
             tile = sb.tile([P, src.shape[2]], I32, name=name, align_bytes=64)
@@ -54,21 +54,29 @@ def tile_picked_yqmix_mix_p_kernel(
             nc.sync.dma_start(tile[:], src.rearrange("(p j) n -> p j n", j=PACK))
             return tile
 
-        def quantize(raw, name):
-            grouped = sb.tile([P, N, PACK], BF16, name=name + "_bf16", align_bytes=64)
-            nc.scalar.copy(grouped[:], raw[:].rearrange("p j n -> p n j"))
-            codes = sb.tile([P, N], U32, name=name + "_codes", align_bytes=64)
-            plane = sb.tile([P, N], U8, name=name + "_plane", align_bytes=64)
+        def interleave(raws, name):
+            grouped = sb.tile([P, len(raws), N, PACK], BF16, name=name + "_bf16", align_bytes=64)
+            for i, raw in enumerate(raws):
+                nc.scalar.copy(
+                    grouped[:, i].rearrange("p (c n) j -> p c j n", n=4),
+                    raw[:].rearrange("p j (c n) -> p c j n", n=4),
+                )
+            return grouped
+
+        def quantize(grouped, name, tag):
+            count = grouped.shape[1]
+            codes = sb.tile([P, count * N], U32, name=name + "_codes", tag=tag, align_bytes=64)
+            plane = sb.tile([P, count * N], U8, name=name + "_plane", align_bytes=64)
             nc.vector.quantize_mx(
-                out=codes[:].bitcast(FP8X4), scales=plane[:], in_=grouped[:].rearrange("p n j -> p (n j)")
+                out=codes[:].bitcast(FP8X4), scales=plane[:], in_=grouped[:].rearrange("p i n j -> p (i n j)")
             )
-            return codes, plane
+            return [(codes[:, i * N : (i + 1) * N], plane[:, i * N : (i + 1) * N]) for i in range(count)]
 
         def product(acc, weight, words, plane):
             nc.tensor.matmul_mx(
                 out=acc,
-                lhsT=weight[0][:].bitcast(FP8X4),
-                lhsT_scale=weight[1][:],
+                lhsT=weight[0].bitcast(FP8X4),
+                lhsT_scale=weight[1],
                 rhs=words.bitcast(FP8X4),
                 rhs_scale=plane,
                 start=True,
@@ -83,19 +91,19 @@ def tile_picked_yqmix_mix_p_kernel(
         nc.vector.memset(zero[:], 0.0)
 
         seen_list = load_list(seen, "seen_list")
-        offs_list = load_list(offs, "offs_list")
-        state_list = load_list(state, "state_list")
-        load_scales(e_plane, e_scales, e_first)
-        load_scales(x_plane, x_scales, x_first)
+        w2_raw = load_weight(w2, "w2_raw")
+        w1_raw = load_weight(w1, "w1_raw")
+        load_scales(e_plane, e_scales, e_first, [nc.sync, nc.sync, nc.scalar, nc.scalar])
         one = sb.tile([P, 1], F32, name="one")
         nc.scalar.activation(one[:], zero[:], ACT.Exp)
-        load_scales(d_plane, d_scales, d_first)
         e_table = load_words(e_words, "e_table")
-        w2_raw = load_weight(w2, "w2_raw")
+        offs_list = load_list(offs, "offs_list")
+        load_scales(x_plane, x_scales, x_first, [nc.sync] * 4)
+        state_list = load_list(state, "state_list")
         x_table = load_words(x_words, "x_table")
-        w1_raw = load_weight(w1, "w1_raw")
-        w3_raw = load_weight(w3, "w3_raw")
+        load_scales(d_plane, d_scales, d_first, [nc.sync] * 4)
         d_table = load_words(d_words, "d_table")
+        w3_raw = load_weight(w3, "w3_raw")
         w4_raw = load_weight(w4, "w4_raw")
 
         e_bytes = sb.tile([P, S], U8, name="e_bytes", align_bytes=64)
@@ -106,47 +114,46 @@ def tile_picked_yqmix_mix_p_kernel(
         d_codes = sb.tile([P, V], U32, name="d_codes", align_bytes=64)
 
         nc.vector.tensor_copy(e_bytes[:], e_plane[:].indirect(seen_list[:]))
+        q2, q1 = quantize(interleave([w2_raw, w1_raw], "w21"), "w21", "e_plane")
         nc.vector.tensor_copy(e_codes[:], e_table[:].bitcast(U32).indirect(seen_list[:]))
-        nc.vector.tensor_copy(x_bytes[:], x_plane[:].indirect(offs_list[:]))
-        q2 = quantize(w2_raw, "w2")
-        nc.vector.tensor_copy(d_bytes[:], d_plane[:].indirect(state_list[:]))
-        nc.vector.tensor_copy(x_codes[:], x_table[:].bitcast(U32).indirect(offs_list[:]))
-
         mix_acc = ps.tile([P, S], F32, name="mix_acc")
         product(mix_acc[:], q2, e_codes[:], e_bytes[e_first:P, :])
         mix = sb.tile([P, D, V], F32, name="mix")
         nc.scalar.activation(mix[:], mix_acc[:].rearrange("p (v d) -> p d v", d=D), ACT.Abs, scale=1.0 / D)
 
-        q1 = quantize(w1_raw, "w1")
+        nc.vector.tensor_copy(x_bytes[:], x_plane[:].indirect(offs_list[:]))
+        nc.vector.tensor_copy(x_codes[:], x_table[:].bitcast(U32).indirect(offs_list[:]))
         val_acc = ps.tile([P, S], F32, name="val_acc")
         product(val_acc[:], q1, x_codes[:], x_bytes[x_first:P, :])
-        q3 = quantize(w3_raw, "w3")
 
-        cols = [slice(h * VH, (h + 1) * VH) for h in range(HALVES)]
-        for h in range(HALVES):
-            part = state_list[:, h * VH // 16 : (h + 1) * VH // 16]
-            nc.vector.tensor_copy(d_codes[:, cols[h]], d_table[:].bitcast(U32).indirect(part))
-        bias_acc = [ps.tile([P, VH], F32, name="bias_acc%d" % h) for h in range(HALVES)]
-        for h in range(HALVES):
-            product(bias_acc[h][:], q3, d_codes[:, cols[h]], d_bytes[d_first:P, cols[h]])
+        nc.vector.tensor_copy(d_bytes[:], d_plane[:].indirect(state_list[:]))
+        nc.vector.tensor_copy(d_codes[:], d_table[:].bitcast(U32).indirect(state_list[:]))
 
-        kq = sb.tile([P, D, V], F32, name="kq")
+        w3_bf16 = interleave([w3_raw], "w3")
+        w4_bf16 = interleave([w4_raw], "w4")
+        (q3,) = quantize(w3_bf16, "w3", "w3_codes")
+        bias_acc = ps.tile([P, V], F32, name="bias_acc")
+        product(bias_acc[:], q3, d_codes[:], d_bytes[d_first:P, :])
+
+        kq = sb.tile([P, D, V], F32, name="kq", tag="w3_raw", align_bytes=64)
         nc.vector.tensor_tensor(kq[:], val_acc[:].rearrange("p (v d) -> p d v", d=D), mix[:], ALU.mult)
-        mean = sb.tile([P, V], F32, name="mean")
-        nc.vector.tensor_tensor(mean[:], kq[:, 0, :], kq[:, 1, :], ALU.add)
 
-        q4 = quantize(w4_raw, "w4")
+        (q4,) = quantize(w4_bf16, "w4", "w4_codes")
         gate_acc = ps.tile([P, V], F32, name="gate_acc")
         product(gate_acc[:], q4, d_codes[:], d_bytes[d_first:P, :])
         gate = sb.tile([P, V], F32, name="gate")
         nc.scalar.activation(gate[:], gate_acc[:], ACT.Abs)
 
         def halves(name):
-            return [sb.tile([P, VH], F32, name="%s%d" % (name, h)) for h in range(HALVES)]
+            return [sb.tile([P, VH], F32, name="%s%d" % (name, h), align_bytes=64) for h in range(HALVES)]
 
-        y, low, ex, elu, res = halves("y"), halves("low"), halves("ex"), halves("elu"), halves("res")
+        cols = [slice(h * VH, (h + 1) * VH) for h in range(HALVES)]
+        mean = sb.tile([P, V], F32, name="mean", tag="w4_raw", align_bytes=64)
+        y, low, ex, elu, res = [halves(n) for n in ("y", "low", "ex", "elu", "res")]
         for h in range(HALVES):
-            nc.vector.tensor_tensor(y[h][:], bias_acc[h][:], mean[:, cols[h]], ALU.add)
+            nc.vector.tensor_tensor(mean[:, cols[h]], kq[:, 0, cols[h]], kq[:, 1, cols[h]], ALU.add)
+        for h in range(HALVES):
+            nc.vector.tensor_tensor(y[h][:], bias_acc[:, cols[h]], mean[:, cols[h]], ALU.add)
         for h in range(HALVES):
             nc.vector.tensor_scalar(low[h][:], y[h][:], 0.0, None, ALU.min)
         for h in range(HALVES):

@@ -19,6 +19,7 @@ P = 128
 PACK = 4
 HALVES = 2
 VH = V // HALVES
+ROWS_AT = P - 16
 
 
 def tile_picked_yqmix_mix_p_kernel(
@@ -34,24 +35,36 @@ def tile_picked_yqmix_mix_p_kernel(
             nc.sync.dma_start(tile[:], src)
             return tile
 
-        def clear_scales(src, name):
+        def load_rows(src, name):
             tile = sb.tile([P, src.shape[2]], U8, name=name, align_bytes=64)
-            nc.vector.memset(tile[:].bitcast(I32), 0)
+            nc.vector.memset(tile[0:ROWS_AT, :].bitcast(I32), 0)
+            nc.sync.dma_start(tile[ROWS_AT:P, :].bitcast(I32), src[0].bitcast(I32))
             return tile
 
-        def load_scales(tile, src, first, queues):
+        def place_rows(rows, name):
+            tile = sb.tile(list(rows.shape), U8, name=name, align_bytes=64)
             for q in range(4):
-                rows = slice(32 * q + first, 32 * q + first + 4)
-                queues[q].dma_start(tile[rows, :].bitcast(I32), src[0, 4 * q : 4 * q + 4, :].bitcast(I32))
+                nc.sync.dma_start(
+                    tile[32 * q : 32 * q + 4, :].bitcast(I32),
+                    rows[ROWS_AT + 4 * q : ROWS_AT + 4 * q + 4, :].bitcast(I32),
+                )
+            return tile
+
+        def load_plane(src, name):
+            tile = sb.tile([P, src.shape[2]], U8, name=name, align_bytes=64)
+            nc.vector.memset(tile[:].bitcast(I32), 0)
+            for q in range(4):
+                nc.sync.dma_start(tile[32 * q : 32 * q + 4, :].bitcast(I32), src[0, 4 * q : 4 * q + 4, :].bitcast(I32))
+            return tile
 
         def load_words(src, name):
             tile = sb.tile([P, src.shape[2]], I32, name=name, align_bytes=64)
             nc.sync.dma_start(tile[:], src[0].rearrange("p n t -> p (n t)").bitcast(I32))
             return tile
 
-        def load_weight(src, name):
+        def load_weight(src, name, queue):
             tile = sb.tile([P, PACK, N], F32, name=name, align_bytes=64)
-            nc.sync.dma_start(tile[:], src.rearrange("(p j) n -> p j n", j=PACK))
+            queue.dma_start(tile[:], src.rearrange("(p j) n -> p j n", j=PACK))
             return tile
 
         def interleave(raws, name):
@@ -83,75 +96,75 @@ def tile_picked_yqmix_mix_p_kernel(
                 stop=True,
             )
 
-        e_first, x_first, d_first = 0, 4, 8
-        e_plane = clear_scales(e_scales, "e_plane")
-        x_plane = clear_scales(x_scales, "x_plane")
-        d_plane = clear_scales(d_scales, "d_plane")
         zero = sb.tile([P, 1], F32, name="zero")
         nc.vector.memset(zero[:], 0.0)
-
-        seen_list = load_list(seen, "seen_list")
-        w2_raw = load_weight(w2, "w2_raw")
-        w1_raw = load_weight(w1, "w1_raw")
-        load_scales(e_plane, e_scales, e_first, [nc.sync, nc.sync, nc.scalar, nc.scalar])
         one = sb.tile([P, 1], F32, name="one")
         nc.scalar.activation(one[:], zero[:], ACT.Exp)
+
+        seen_list = load_list(seen, "seen_list")
+        e_rows = load_rows(e_scales, "e_rows")
+        w2_raw = load_weight(w2, "w2_raw", nc.scalar)
+        state_list = load_list(state, "state_list")
+        d_rows = load_rows(d_scales, "d_rows")
         e_table = load_words(e_words, "e_table")
         offs_list = load_list(offs, "offs_list")
-        load_scales(x_plane, x_scales, x_first, [nc.sync] * 4)
-        state_list = load_list(state, "state_list")
+        x_plane = load_plane(x_scales, "x_plane")
         x_table = load_words(x_words, "x_table")
-        load_scales(d_plane, d_scales, d_first, [nc.sync] * 4)
-        d_table = load_words(d_words, "d_table")
-        w3_raw = load_weight(w3, "w3_raw")
-        w4_raw = load_weight(w4, "w4_raw")
 
-        e_bytes = sb.tile([P, S], U8, name="e_bytes", align_bytes=64)
+        e_picked = sb.tile([P, S], U8, name="e_picked", align_bytes=64)
         e_codes = sb.tile([P, S], U32, name="e_codes", align_bytes=64)
         x_bytes = sb.tile([P, S], U8, name="x_bytes", align_bytes=64)
         x_codes = sb.tile([P, S], U32, name="x_codes", align_bytes=64)
-        d_bytes = sb.tile([P, V], U8, name="d_bytes", align_bytes=64)
+        d_picked = sb.tile([P, V], U8, name="d_picked", align_bytes=64)
         d_codes = sb.tile([P, V], U32, name="d_codes", align_bytes=64)
 
-        nc.vector.tensor_copy(e_bytes[:], e_plane[:].indirect(seen_list[:]))
-        q2, q1 = quantize(interleave([w2_raw, w1_raw], "w21"), "w21", "e_plane")
-        nc.vector.tensor_copy(e_codes[:], e_table[:].bitcast(U32).indirect(seen_list[:]))
-        mix_acc = ps.tile([P, S], F32, name="mix_acc")
-        product(mix_acc[:], q2, e_codes[:], e_bytes[e_first:P, :])
-        mix = sb.tile([P, D, V], F32, name="mix")
-        nc.scalar.activation(mix[:], mix_acc[:].rearrange("p (v d) -> p d v", d=D), ACT.Abs, scale=1.0 / D)
+        nc.vector.tensor_copy(e_picked[:], e_rows[:].indirect(seen_list[:]))
+        (q2,) = quantize(interleave([w2_raw], "w2"), "w2", "w2_codes")
+        nc.vector.tensor_copy(d_picked[:], d_rows[:].indirect(state_list[:]))
 
+        e_bytes = place_rows(e_picked, "e_bytes")
+        w1_raw = load_weight(w1, "w1_raw", nc.sync)
+        d_table = load_words(d_words, "d_table")
+        w3_raw = load_weight(w3, "w3_raw", nc.sync)
+        w4_raw = load_weight(w4, "w4_raw", nc.sync)
+        d_bytes = place_rows(d_picked, "d_bytes")
+
+        nc.vector.tensor_copy(e_codes[:], e_table[:].bitcast(U32).indirect(seen_list[:]))
         nc.vector.tensor_copy(x_bytes[:], x_plane[:].indirect(offs_list[:]))
         nc.vector.tensor_copy(x_codes[:], x_table[:].bitcast(U32).indirect(offs_list[:]))
+        mix_acc = ps.tile([P, S], F32, name="mix_acc")
+        product(mix_acc[:], q2, e_codes[:], e_bytes[:])
+        (q1,) = quantize(interleave([w1_raw], "w1"), "w1", "w1_codes")
         val_acc = ps.tile([P, S], F32, name="val_acc")
-        product(val_acc[:], q1, x_codes[:], x_bytes[x_first:P, :])
+        product(val_acc[:], q1, x_codes[:], x_bytes[:])
+        mix = sb.tile([P, D, V], F32, name="mix", tag="w1_raw", align_bytes=64)
+        nc.scalar.activation(mix[:], mix_acc[:].rearrange("p (v d) -> p d v", d=D), ACT.Abs, scale=1.0 / D)
 
-        nc.vector.tensor_copy(d_bytes[:], d_plane[:].indirect(state_list[:]))
         nc.vector.tensor_copy(d_codes[:], d_table[:].bitcast(U32).indirect(state_list[:]))
+        kq = sb.tile([P, D, V], F32, name="kq", align_bytes=64)
+        nc.vector.tensor_tensor(kq[:], val_acc[:].rearrange("p (v d) -> p d v", d=D), mix[:], ALU.mult)
 
         w3_bf16 = interleave([w3_raw], "w3")
         w4_bf16 = interleave([w4_raw], "w4")
         (q3,) = quantize(w3_bf16, "w3", "w3_codes")
         bias_acc = ps.tile([P, V], F32, name="bias_acc")
-        product(bias_acc[:], q3, d_codes[:], d_bytes[d_first:P, :])
-
-        kq = sb.tile([P, D, V], F32, name="kq", tag="w3_raw", align_bytes=64)
-        nc.vector.tensor_tensor(kq[:], val_acc[:].rearrange("p (v d) -> p d v", d=D), mix[:], ALU.mult)
-
-        (q4,) = quantize(w4_bf16, "w4", "w4_codes")
-        gate_acc = ps.tile([P, V], F32, name="gate_acc")
-        product(gate_acc[:], q4, d_codes[:], d_bytes[d_first:P, :])
-        gate = sb.tile([P, V], F32, name="gate")
-        nc.scalar.activation(gate[:], gate_acc[:], ACT.Abs)
+        product(bias_acc[:], q3, d_codes[:], d_bytes[:])
 
         def halves(name):
             return [sb.tile([P, VH], F32, name="%s%d" % (name, h), align_bytes=64) for h in range(HALVES)]
 
         cols = [slice(h * VH, (h + 1) * VH) for h in range(HALVES)]
-        mean = sb.tile([P, V], F32, name="mean", tag="w4_raw", align_bytes=64)
-        y, low, ex, elu, res = [halves(n) for n in ("y", "low", "ex", "elu", "res")]
+        mean = sb.tile([P, V], F32, name="mean", tag="w3_raw", align_bytes=64)
         for h in range(HALVES):
             nc.vector.tensor_tensor(mean[:, cols[h]], kq[:, 0, cols[h]], kq[:, 1, cols[h]], ALU.add)
+
+        (q4,) = quantize(w4_bf16, "w4", "w4_codes")
+        gate_acc = ps.tile([P, V], F32, name="gate_acc")
+        product(gate_acc[:], q4, d_codes[:], d_bytes[:])
+        gate = sb.tile([P, V], F32, name="gate")
+        nc.scalar.activation(gate[:], gate_acc[:], ACT.Abs)
+
+        y, low, ex, elu, res = [halves(n) for n in ("y", "low", "ex", "elu", "res")]
         for h in range(HALVES):
             nc.vector.tensor_tensor(y[h][:], bias_acc[:, cols[h]], mean[:, cols[h]], ALU.add)
         for h in range(HALVES):

@@ -17,6 +17,7 @@ ACT = mybir.ActivationFunctionType
 
 P = 128
 PACK = 4
+QUADRANTS = 4
 HALVES = 2
 VH = V // HALVES
 ROWS_AT = P - 16
@@ -38,23 +39,7 @@ def tile_picked_yqmix_mix_p_kernel(
         def load_rows(src, name):
             tile = sb.tile([P, src.shape[2]], U8, name=name, align_bytes=64)
             nc.vector.memset(tile[0:ROWS_AT, :].bitcast(I32), 0)
-            nc.sync.dma_start(tile[ROWS_AT:P, :].bitcast(I32), src[0].bitcast(I32))
-            return tile
-
-        def place_rows(rows, name):
-            tile = sb.tile(list(rows.shape), U8, name=name, align_bytes=64)
-            for q in range(4):
-                nc.sync.dma_start(
-                    tile[32 * q : 32 * q + 4, :].bitcast(I32),
-                    rows[ROWS_AT + 4 * q : ROWS_AT + 4 * q + 4, :].bitcast(I32),
-                )
-            return tile
-
-        def load_plane(src, name):
-            tile = sb.tile([P, src.shape[2]], U8, name=name, align_bytes=64)
-            nc.vector.memset(tile[:].bitcast(I32), 0)
-            for q in range(4):
-                nc.sync.dma_start(tile[32 * q : 32 * q + 4, :].bitcast(I32), src[0, 4 * q : 4 * q + 4, :].bitcast(I32))
+            nc.scalar.dma_start(tile[ROWS_AT:P, :].bitcast(I32), src[0].bitcast(I32))
             return tile
 
         def load_words(src, name):
@@ -67,112 +52,115 @@ def tile_picked_yqmix_mix_p_kernel(
             queue.dma_start(tile[:], src.rearrange("(p j) n -> p j n", j=PACK))
             return tile
 
-        def interleave(raws, name):
-            grouped = sb.tile([P, len(raws), N, PACK], BF16, name=name + "_bf16", align_bytes=64)
-            for i, raw in enumerate(raws):
-                nc.scalar.copy(
-                    grouped[:, i].rearrange("p (c n) j -> p c j n", n=4),
-                    raw[:].rearrange("p j (c n) -> p c j n", n=4),
-                )
+        def interleave(raw, name):
+            grouped = sb.tile([P, N, PACK], BF16, name=name + "_bf16", align_bytes=64)
+            nc.scalar.copy(
+                grouped[:].rearrange("p (c n) j -> p c j n", n=4),
+                raw[:].rearrange("p j (c n) -> p c j n", n=4),
+            )
             return grouped
 
-        def quantize(grouped, name, tag):
-            count = grouped.shape[1]
-            codes = sb.tile([P, count * N], U32, name=name + "_codes", tag=tag, align_bytes=64)
-            plane = sb.tile([P, count * N], U8, name=name + "_plane", align_bytes=64)
+        def quantize(grouped, name):
+            codes = sb.tile([P, N], U32, name=name + "_codes", align_bytes=64)
+            plane = sb.tile([P, N], U8, name=name + "_plane", align_bytes=64)
             nc.vector.quantize_mx(
-                out=codes[:].bitcast(FP8X4), scales=plane[:], in_=grouped[:].rearrange("p i n j -> p (i n j)")
+                out=codes[:].bitcast(FP8X4), scales=plane[:], in_=grouped[:].rearrange("p n j -> p (n j)")
             )
-            return [(codes[:, i * N : (i + 1) * N], plane[:, i * N : (i + 1) * N]) for i in range(count)]
+            return codes, plane
+
+        def gather_words(table, entries, name):
+            codes = sb.tile([P, 16 * entries.shape[1]], U32, name=name, align_bytes=64)
+            nc.vector.tensor_copy(codes[:], table[:].bitcast(U32).indirect(entries))
+            return codes
 
         def product(acc, weight, words, plane):
             nc.tensor.matmul_mx(
                 out=acc,
-                lhsT=weight[0].bitcast(FP8X4),
-                lhsT_scale=weight[1],
+                lhsT=weight[0][:].bitcast(FP8X4),
+                lhsT_scale=weight[1][:],
                 rhs=words.bitcast(FP8X4),
                 rhs_scale=plane,
                 start=True,
                 stop=True,
             )
 
+        seen_list = load_list(seen, "seen_list")
+        e_rows = load_rows(e_scales, "e_rows")
+        offs_list = load_list(offs, "offs_list")
+        x_rows = load_rows(x_scales, "x_rows")
+        state_list = load_list(state, "state_list")
+        d_rows = load_rows(d_scales, "d_rows")
+        e_table = load_words(e_words, "e_table")
+        w2_raw = load_weight(w2, "w2_raw", nc.scalar)
+        w1_raw = load_weight(w1, "w1_raw", nc.sync)
+        x_table = load_words(x_words, "x_table")
+
         zero = sb.tile([P, 1], F32, name="zero")
         nc.vector.memset(zero[:], 0.0)
         one = sb.tile([P, 1], F32, name="one")
         nc.scalar.activation(one[:], zero[:], ACT.Exp)
 
-        seen_list = load_list(seen, "seen_list")
-        e_rows = load_rows(e_scales, "e_rows")
-        w2_raw = load_weight(w2, "w2_raw", nc.scalar)
-        state_list = load_list(state, "state_list")
-        d_rows = load_rows(d_scales, "d_rows")
-        e_table = load_words(e_words, "e_table")
-        offs_list = load_list(offs, "offs_list")
-        x_plane = load_plane(x_scales, "x_plane")
-        x_table = load_words(x_words, "x_table")
-
-        e_picked = sb.tile([P, S], U8, name="e_picked", align_bytes=64)
-        e_codes = sb.tile([P, S], U32, name="e_codes", align_bytes=64)
-        x_bytes = sb.tile([P, S], U8, name="x_bytes", align_bytes=64)
-        x_codes = sb.tile([P, S], U32, name="x_codes", align_bytes=64)
-        d_picked = sb.tile([P, V], U8, name="d_picked", align_bytes=64)
-        d_codes = sb.tile([P, V], U32, name="d_codes", align_bytes=64)
-
-        nc.vector.tensor_copy(e_picked[:], e_rows[:].indirect(seen_list[:]))
-        (q2,) = quantize(interleave([w2_raw], "w2"), "w2", "w2_codes")
-        nc.vector.tensor_copy(d_picked[:], d_rows[:].indirect(state_list[:]))
-
-        e_bytes = place_rows(e_picked, "e_bytes")
-        w1_raw = load_weight(w1, "w1_raw", nc.sync)
-        d_table = load_words(d_words, "d_table")
+        picked = sb.tile([P, 2 * S + V], U8, name="picked", align_bytes=64)
+        e_at, x_at, d_at = 0, S, 2 * S
+        nc.vector.tensor_copy(picked[:, e_at : e_at + S], e_rows[:].indirect(seen_list[:]))
+        nc.vector.tensor_copy(picked[:, x_at : x_at + S], x_rows[:].indirect(offs_list[:]))
+        nc.vector.tensor_copy(picked[:, d_at : d_at + V], d_rows[:].indirect(state_list[:]))
+        planes = sb.tile([P, 2 * S + V], U8, name="planes", align_bytes=64)
+        for q in range(QUADRANTS):
+            nc.sync.dma_start(
+                planes[32 * q : 32 * q + 4, :].bitcast(I32),
+                picked[ROWS_AT + 4 * q : ROWS_AT + 4 * q + 4, :].bitcast(I32),
+            )
         w3_raw = load_weight(w3, "w3_raw", nc.sync)
+        d_table = load_words(d_words, "d_table")
         w4_raw = load_weight(w4, "w4_raw", nc.sync)
-        d_bytes = place_rows(d_picked, "d_bytes")
 
-        nc.vector.tensor_copy(e_codes[:], e_table[:].bitcast(U32).indirect(seen_list[:]))
-        nc.vector.tensor_copy(x_bytes[:], x_plane[:].indirect(offs_list[:]))
-        nc.vector.tensor_copy(x_codes[:], x_table[:].bitcast(U32).indirect(offs_list[:]))
-        mix_acc = ps.tile([P, S], F32, name="mix_acc")
-        product(mix_acc[:], q2, e_codes[:], e_bytes[:])
-        (q1,) = quantize(interleave([w1_raw], "w1"), "w1", "w1_codes")
-        val_acc = ps.tile([P, S], F32, name="val_acc")
-        product(val_acc[:], q1, x_codes[:], x_bytes[:])
-        mix = sb.tile([P, D, V], F32, name="mix", tag="w1_raw", align_bytes=64)
-        nc.scalar.activation(mix[:], mix_acc[:].rearrange("p (v d) -> p d v", d=D), ACT.Abs, scale=1.0 / D)
+        q2 = quantize(interleave(w2_raw, "w2"), "w2")
+        e_codes = gather_words(e_table, seen_list[:], "e_codes")
+        q1 = quantize(interleave(w1_raw, "w1"), "w1")
 
-        nc.vector.tensor_copy(d_codes[:], d_table[:].bitcast(U32).indirect(state_list[:]))
-        kq = sb.tile([P, D, V], F32, name="kq", align_bytes=64)
-        nc.vector.tensor_tensor(kq[:], val_acc[:].rearrange("p (v d) -> p d v", d=D), mix[:], ALU.mult)
+        def halves(name, shape, pool=sb):
+            return [pool.tile(shape, F32, name="%s%d" % (name, h)) for h in range(HALVES)]
 
-        w3_bf16 = interleave([w3_raw], "w3")
-        w4_bf16 = interleave([w4_raw], "w4")
-        (q3,) = quantize(w3_bf16, "w3", "w3_codes")
-        bias_acc = ps.tile([P, V], F32, name="bias_acc")
-        product(bias_acc[:], q3, d_codes[:], d_bytes[:])
+        SH = S // HALVES
+        both = range(HALVES)
+        x_codes = [gather_words(x_table, offs_list[:, h * SH // 16 : (h + 1) * SH // 16], "x_codes%d" % h) for h in both]
+        mix_acc, val_acc = halves("mix_acc", [P, SH], ps), halves("val_acc", [P, SH], ps)
+        for h in both:
+            product(mix_acc[h][:], q2, e_codes[:, h * SH : (h + 1) * SH], planes[:, e_at + h * SH : e_at + (h + 1) * SH])
+            product(val_acc[h][:], q1, x_codes[h][:], planes[:, x_at + h * SH : x_at + (h + 1) * SH])
+        q3 = quantize(interleave(w3_raw, "w3"), "w3")
+        mix = sb.tile([P, HALVES, D, VH], F32, name="mix", tag="w3_raw", align_bytes=64)
+        for h in both:
+            nc.scalar.activation(mix[:, h], mix_acc[h][:].rearrange("p (v d) -> p d v", d=D), ACT.Abs, scale=1.0 / D)
 
-        def halves(name):
-            return [sb.tile([P, VH], F32, name="%s%d" % (name, h), align_bytes=64) for h in range(HALVES)]
+        kq = halves("kq", [P, D, VH])
+        bias_acc, gate_acc = halves("bias_acc", [P, VH], ps), halves("gate_acc", [P, VH], ps)
+        d_codes = []
+        for h in both:
+            d_codes.append(gather_words(d_table, state_list[:, h * VH // 16 : (h + 1) * VH // 16], "d_codes%d" % h))
+            product(bias_acc[h][:], q3, d_codes[h][:], planes[:, d_at + h * VH : d_at + (h + 1) * VH])
+            nc.vector.tensor_tensor(kq[h][:], val_acc[h][:].rearrange("p (v d) -> p d v", d=D), mix[:, h], ALU.mult)
 
-        cols = [slice(h * VH, (h + 1) * VH) for h in range(HALVES)]
-        mean = sb.tile([P, V], F32, name="mean", tag="w3_raw", align_bytes=64)
-        for h in range(HALVES):
-            nc.vector.tensor_tensor(mean[:, cols[h]], kq[:, 0, cols[h]], kq[:, 1, cols[h]], ALU.add)
-
-        (q4,) = quantize(w4_bf16, "w4", "w4_codes")
-        gate_acc = ps.tile([P, V], F32, name="gate_acc")
-        product(gate_acc[:], q4, d_codes[:], d_bytes[:])
-        gate = sb.tile([P, V], F32, name="gate")
-        nc.scalar.activation(gate[:], gate_acc[:], ACT.Abs)
-
-        y, low, ex, elu, res = [halves(n) for n in ("y", "low", "ex", "elu", "res")]
-        for h in range(HALVES):
-            nc.vector.tensor_tensor(y[h][:], bias_acc[:, cols[h]], mean[:, cols[h]], ALU.add)
-        for h in range(HALVES):
-            nc.vector.tensor_scalar(low[h][:], y[h][:], 0.0, None, ALU.min)
-        for h in range(HALVES):
+        w4_bf16 = interleave(w4_raw, "w4")
+        mean, gate, low, ex, elu, res = [halves(n, [P, VH]) for n in ("mean", "gate", "low", "ex", "elu", "res")]
+        y_both = sb.tile([P, HALVES, VH], F32, name="y_both", tag="w4_raw", align_bytes=64)
+        y = [y_both[:, h] for h in both]
+        for h in both:
+            nc.vector.tensor_tensor(mean[h][:], kq[h][:, 0, :], kq[h][:, 1, :], ALU.add)
+        q4 = quantize(w4_bf16, "w4")
+        for h in both:
+            product(gate_acc[h][:], q4, d_codes[h][:], planes[:, d_at + h * VH : d_at + (h + 1) * VH])
+        for h in both:
+            nc.vector.tensor_tensor(y[h], bias_acc[h][:], mean[h][:], ALU.add)
+        for h in both:
+            nc.vector.tensor_scalar(low[h][:], y[h], 0.0, None, ALU.min)
+        for h in both:
             nc.scalar.activation(ex[h][:], low[h][:], ACT.Exp)
-        for h in range(HALVES):
-            nc.vector.scalar_tensor_tensor(elu[h][:], ex[h][:], one[:], y[h][:], ALU.subtract, ALU.max)
-        for h in range(HALVES):
-            nc.vector.tensor_tensor(res[h][:], elu[h][:], gate[:, cols[h]], ALU.mult)
-            nc.sync.dma_start(out[:, cols[h]], res[h][:])
+        for h in both:
+            nc.scalar.activation(gate[h][:], gate_acc[h][:], ACT.Abs)
+        for h in both:
+            nc.vector.scalar_tensor_tensor(elu[h][:], ex[h][:], one[:], y[h], ALU.subtract, ALU.max)
+        for h in both:
+            nc.vector.tensor_tensor(res[h][:], elu[h][:], gate[h][:], ALU.mult)
+            nc.sync.dma_start(out[:, h * VH : (h + 1) * VH], res[h][:])

@@ -106,11 +106,8 @@ def tile_picked_yqmix_mix_p_kernel(
         nc.vector.tensor_copy(picked[:, x_at : x_at + S], x_rows[:].indirect(offs_list[:]))
         nc.vector.tensor_copy(picked[:, d_at : d_at + V], d_rows[:].indirect(state_list[:]))
         planes = sb.tile([P, 2 * S + V], U8, name="planes", align_bytes=64)
-        for q in range(QUADRANTS):
-            nc.sync.dma_start(
-                planes[32 * q : 32 * q + 4, :].bitcast(I32),
-                picked[ROWS_AT + 4 * q : ROWS_AT + 4 * q + 4, :].bitcast(I32),
-            )
+        for r in range(4):
+            nc.sync.dma_start(planes[r:P:32, :].bitcast(I32), picked[ROWS_AT + r : P : 4, :].bitcast(I32))
         w3_raw = load_weight(w3, "w3_raw", nc.sync)
         d_table = load_words(d_words, "d_table")
         w4_raw = load_weight(w4, "w4_raw", nc.sync)

@@ -140,7 +140,8 @@ def tile_picked_yqmix_mix_p_kernel(
             nc.vector.tensor_tensor(kq[h][:], val_acc[h][:].rearrange("p (v d) -> p d v", d=D), mix[:, h], ALU.mult)
 
         w4_bf16 = interleave(w4_raw, "w4")
-        mean, gate, low, ex, elu, res = [halves(n, [P, VH]) for n in ("mean", "gate", "low", "ex", "elu", "res")]
+        mean, gate, low, ex, elu = [halves(n, [P, VH]) for n in ("mean", "gate", "low", "ex", "elu")]
+        res = sb.tile([P, V], F32, name="res")
         y_both = sb.tile([P, HALVES, VH], F32, name="y_both", tag="w4_raw", align_bytes=64)
         y = [y_both[:, h] for h in both]
         for h in both:
@@ -159,5 +160,5 @@ def tile_picked_yqmix_mix_p_kernel(
         for h in both:
             nc.vector.scalar_tensor_tensor(elu[h][:], ex[h][:], one[:], y[h], ALU.subtract, ALU.max)
         for h in both:
-            nc.vector.tensor_tensor(res[h][:], elu[h][:], gate[h][:], ALU.mult)
-            nc.sync.dma_start(out[:, h * VH : (h + 1) * VH], res[h][:])
+            nc.vector.tensor_tensor(res[:, h * VH : (h + 1) * VH], elu[h][:], gate[h][:], ALU.mult)
+        nc.sync.dma_start(out, res[:])

@@ -137,6 +137,7 @@ def tile_picked_yqmix_mix_p_kernel(
         for h in both:
             d_codes.append(gather_words(d_table, state_list[:, h * VH // 16 : (h + 1) * VH // 16], "d_codes%d" % h))
             product(bias_acc[h][:], q3, d_codes[h][:], planes[:, d_at + h * VH : d_at + (h + 1) * VH])
+        for h in both:
             nc.vector.tensor_tensor(kq[h][:], val_acc[h][:].rearrange("p (v d) -> p d v", d=D), mix[:, h], ALU.mult)
 
         w4_bf16 = interleave(w4_raw, "w4")

@@ -84,12 +84,12 @@ def tile_picked_yqmix_mix_p_kernel(
                 stop=True,
             )
 
+        state_list = load_list(state, "state_list")
+        d_rows = load_rows(d_scales, "d_rows")
         seen_list = load_list(seen, "seen_list")
         e_rows = load_rows(e_scales, "e_rows")
         offs_list = load_list(offs, "offs_list")
         x_rows = load_rows(x_scales, "x_rows")
-        state_list = load_list(state, "state_list")
-        d_rows = load_rows(d_scales, "d_rows")
         e_table = load_words(e_words, "e_table")
         w2_raw = load_weight(w2, "w2_raw", nc.scalar)
         w1_raw = load_weight(w1, "w1_raw", nc.sync)
@@ -102,9 +102,9 @@ def tile_picked_yqmix_mix_p_kernel(
 
         picked = sb.tile([P, 2 * S + V], U8, name="picked", align_bytes=64)
         e_at, x_at, d_at = 0, S, 2 * S
+        nc.vector.tensor_copy(picked[:, d_at : d_at + V], d_rows[:].indirect(state_list[:]))
         nc.vector.tensor_copy(picked[:, e_at : e_at + S], e_rows[:].indirect(seen_list[:]))
         nc.vector.tensor_copy(picked[:, x_at : x_at + S], x_rows[:].indirect(offs_list[:]))
-        nc.vector.tensor_copy(picked[:, d_at : d_at + V], d_rows[:].indirect(state_list[:]))
         planes = sb.tile([P, 2 * S + V], U8, name="planes", align_bytes=64)
         for r in range(4):
             nc.sync.dma_start(planes[r:P:32, :].bitcast(I32), picked[ROWS_AT + r : P : 4, :].bitcast(I32))
@@ -132,14 +132,13 @@ def tile_picked_yqmix_mix_p_kernel(
             nc.scalar.activation(mix[:, h], mix_acc[h][:].rearrange("p (v d) -> p d v", d=D), ACT.Abs, scale=1.0 / D)
 
         kq = halves("kq", [P, D, VH])
-        bias_acc, gate_acc = halves("bias_acc", [P, VH], ps), halves("gate_acc", [P, VH], ps)
-        d_codes = []
-        for h in both:
-            d_codes.append(gather_words(d_table, state_list[:, h * VH // 16 : (h + 1) * VH // 16], "d_codes%d" % h))
-            product(bias_acc[h][:], q3, d_codes[h][:], planes[:, d_at + h * VH : d_at + (h + 1) * VH])
+        d_codes = gather_words(d_table, state_list[:], "d_codes")
+        bias_acc = ps.tile([P, V], F32, name="bias_acc")
+        product(bias_acc[:], q3, d_codes[:], planes[:, d_at : d_at + V])
         for h in both:
             nc.vector.tensor_tensor(kq[h][:], val_acc[h][:].rearrange("p (v d) -> p d v", d=D), mix[:, h], ALU.mult)
 
+        gate_acc = halves("gate_acc", [P, VH], ps)
         w4_bf16 = interleave(w4_raw, "w4")
         mean, gate, low, ex, elu = [halves(n, [P, VH]) for n in ("mean", "gate", "low", "ex", "elu")]
         res = sb.tile([P, V], F32, name="res")
@@ -149,9 +148,9 @@ def tile_picked_yqmix_mix_p_kernel(
             nc.vector.tensor_tensor(mean[h][:], kq[h][:, 0, :], kq[h][:, 1, :], ALU.add)
         q4 = quantize(w4_bf16, "w4")
         for h in both:
-            product(gate_acc[h][:], q4, d_codes[h][:], planes[:, d_at + h * VH : d_at + (h + 1) * VH])
+            product(gate_acc[h][:], q4, d_codes[:, h * VH : (h + 1) * VH], planes[:, d_at + h * VH : d_at + (h + 1) * VH])
         for h in both:
-            nc.vector.tensor_tensor(y[h], bias_acc[h][:], mean[h][:], ALU.add)
+            nc.vector.tensor_tensor(y[h], bias_acc[:, h * VH : (h + 1) * VH], mean[h][:], ALU.add)
         for h in both:
             nc.vector.tensor_scalar(low[h][:], y[h], 0.0, None, ALU.min)
         for h in both:

@@ -140,25 +140,25 @@ def tile_picked_yqmix_mix_p_kernel(
 
         gate_acc = halves("gate_acc", [P, VH], ps)
         w4_bf16 = interleave(w4_raw, "w4")
-        mean, gate, low, ex, elu = [halves(n, [P, VH]) for n in ("mean", "gate", "low", "ex", "elu")]
+        mean, y, gate, ex, elu = [halves(n, [P, VH]) for n in ("mean", "y", "gate", "ex", "elu")]
         res = sb.tile([P, V], F32, name="res")
-        y_both = sb.tile([P, HALVES, VH], F32, name="y_both", tag="w4_raw", align_bytes=64)
-        y = [y_both[:, h] for h in both]
+        low_both = sb.tile([P, HALVES, VH], F32, name="low_both", tag="w4_raw", align_bytes=64)
+        low = [low_both[:, h] for h in both]
         for h in both:
             nc.vector.tensor_tensor(mean[h][:], kq[h][:, 0, :], kq[h][:, 1, :], ALU.add)
+        for h in both:
+            nc.vector.tensor_tensor(y[h][:], bias_acc[:, h * VH : (h + 1) * VH], mean[h][:], ALU.add)
         q4 = quantize(w4_bf16, "w4")
         for h in both:
             product(gate_acc[h][:], q4, d_codes[:, h * VH : (h + 1) * VH], planes[:, d_at + h * VH : d_at + (h + 1) * VH])
         for h in both:
-            nc.vector.tensor_tensor(y[h], bias_acc[:, h * VH : (h + 1) * VH], mean[h][:], ALU.add)
+            nc.vector.tensor_scalar(low[h], y[h][:], 0.0, None, ALU.min)
         for h in both:
-            nc.vector.tensor_scalar(low[h][:], y[h], 0.0, None, ALU.min)
-        for h in both:
-            nc.scalar.activation(ex[h][:], low[h][:], ACT.Exp)
+            nc.scalar.activation(ex[h][:], low[h], ACT.Exp)
         for h in both:
             nc.scalar.activation(gate[h][:], gate_acc[h][:], ACT.Abs)
         for h in both:
-            nc.vector.scalar_tensor_tensor(elu[h][:], ex[h][:], one[:], y[h], ALU.subtract, ALU.max)
+            nc.vector.scalar_tensor_tensor(elu[h][:], ex[h][:], one[:], y[h][:], ALU.subtract, ALU.max)
         for h in both:
             nc.vector.tensor_tensor(res[:, h * VH : (h + 1) * VH], elu[h][:], gate[h][:], ALU.mult)
         nc.sync.dma_start(out, res[:])

@@ -141,7 +141,7 @@ def tile_picked_yqmix_mix_p_kernel(
         gate_acc = halves("gate_acc", [P, VH], ps)
         w4_bf16 = interleave(w4_raw, "w4")
         mean, y, gate, ex, elu = [halves(n, [P, VH]) for n in ("mean", "y", "gate", "ex", "elu")]
-        res = sb.tile([P, V], F32, name="res")
+        res = halves("res", [P, VH])
         low_both = sb.tile([P, HALVES, VH], F32, name="low_both", tag="w4_raw", align_bytes=64)
         low = [low_both[:, h] for h in both]
         for h in both:
@@ -160,5 +160,5 @@ def tile_picked_yqmix_mix_p_kernel(
         for h in both:
             nc.vector.scalar_tensor_tensor(elu[h][:], ex[h][:], one[:], y[h][:], ALU.subtract, ALU.max)
         for h in both:
-            nc.vector.tensor_tensor(res[:, h * VH : (h + 1) * VH], elu[h][:], gate[h][:], ALU.mult)
-        nc.sync.dma_start(out, res[:])
+            nc.vector.tensor_tensor(res[h][:], elu[h][:], gate[h][:], ALU.mult)
+            (nc.scalar, nc.sync)[h].dma_start(out[:, h * VH : (h + 1) * VH], res[h][:])

from contextlib import ExitStack

import concourse.mybir as mybir

K, N, S, V, D = 512, 128, 512, 256, 2
FLOPS = 2 * K * N * (2 * S + 2 * V)

F32 = mybir.dt.float32
BF16 = mybir.dt.bfloat16
I32 = mybir.dt.int32
U32 = mybir.dt.uint32
U16 = mybir.dt.uint16
U8 = mybir.dt.uint8
FP8X4 = mybir.dt.float8_e4m3fn_x4
ALU = mybir.AluOpType
ACT = mybir.ActivationFunctionType

P = 128
PACK = 4
QUADRANTS = 4
HALVES = 2
VH = V // HALVES
ROWS_AT = P - 16


def tile_picked_yqmix_mix_p_kernel(
    tc, x_words, x_scales, e_words, e_scales, d_words, d_scales, w1, w2, w3, w4, offs, seen, state, out
):
    nc = tc.nc
    with ExitStack() as ctx:
        sb = ctx.enter_context(tc.tile_pool(name="sb", bufs=1))
        ps = ctx.enter_context(tc.psum_pool(name="ps", bufs=1))

        def load_list(src, name):
            tile = sb.tile(list(src.shape), U16, name=name)
            nc.sync.dma_start(tile[:], src)
            return tile

        def load_rows(src, name):
            tile = sb.tile([P, src.shape[2]], U8, name=name, align_bytes=64)
            nc.vector.memset(tile[0:ROWS_AT, :].bitcast(I32), 0)
            nc.scalar.dma_start(tile[ROWS_AT:P, :].bitcast(I32), src[0].bitcast(I32))
            return tile

        def load_words(src, name):
            tile = sb.tile([P, src.shape[2]], I32, name=name, align_bytes=64)
            nc.sync.dma_start(tile[:], src[0].rearrange("p n t -> p (n t)").bitcast(I32))
            return tile

        def load_weight(src, name, queue):
            tile = sb.tile([P, PACK, N], F32, name=name, align_bytes=64)
            queue.dma_start(tile[:], src.rearrange("(p j) n -> p j n", j=PACK))
            return tile

        def interleave(raw, name):
            grouped = sb.tile([P, N, PACK], BF16, name=name + "_bf16", align_bytes=64)
            nc.scalar.copy(
                grouped[:].rearrange("p (c n) j -> p c j n", n=4),
                raw[:].rearrange("p j (c n) -> p c j n", n=4),
            )
            return grouped

        def quantize(grouped, name):
            codes = sb.tile([P, N], U32, name=name + "_codes", align_bytes=64)
            plane = sb.tile([P, N], U8, name=name + "_plane", align_bytes=64)
            nc.vector.quantize_mx(
                out=codes[:].bitcast(FP8X4), scales=plane[:], in_=grouped[:].rearrange("p n j -> p (n j)")
            )
            return codes, plane

        def gather_words(table, entries, name):
            codes = sb.tile([P, 16 * entries.shape[1]], U32, name=name, align_bytes=64)
            nc.vector.tensor_copy(codes[:], table[:].bitcast(U32).indirect(entries))
            return codes

        def product(acc, weight, words, plane):
            nc.tensor.matmul_mx(
                out=acc,
                lhsT=weight[0][:].bitcast(FP8X4),
                lhsT_scale=weight[1][:],
                rhs=words.bitcast(FP8X4),
                rhs_scale=plane,
                start=True,
                stop=True,
            )

        state_list = load_list(state, "state_list")
        d_rows = load_rows(d_scales, "d_rows")
        seen_list = load_list(seen, "seen_list")
        e_rows = load_rows(e_scales, "e_rows")
        offs_list = load_list(offs, "offs_list")
        x_rows = load_rows(x_scales, "x_rows")
        e_table = load_words(e_words, "e_table")
        w2_raw = load_weight(w2, "w2_raw", nc.scalar)
        w1_raw = load_weight(w1, "w1_raw", nc.sync)
        x_table = load_words(x_words, "x_table")

        zero = sb.tile([P, 1], F32, name="zero")
        nc.vector.memset(zero[:], 0.0)
        one = sb.tile([P, 1], F32, name="one")
        nc.scalar.activation(one[:], zero[:], ACT.Exp)

        picked = sb.tile([P, 2 * S + V], U8, name="picked", align_bytes=64)
        e_at, x_at, d_at = 0, S, 2 * S
        nc.vector.tensor_copy(picked[:, d_at : d_at + V], d_rows[:].indirect(state_list[:]))
        nc.vector.tensor_copy(picked[:, e_at : e_at + S], e_rows[:].indirect(seen_list[:]))
        nc.vector.tensor_copy(picked[:, x_at : x_at + S], x_rows[:].indirect(offs_list[:]))
        planes = sb.tile([P, 2 * S + V], U8, name="planes", align_bytes=64)
        for r in range(4):
            nc.sync.dma_start(planes[r:P:32, :].bitcast(I32), picked[ROWS_AT + r : P : 4, :].bitcast(I32))
        w3_raw = load_weight(w3, "w3_raw", nc.sync)
        d_table = load_words(d_words, "d_table")
        w4_raw = load_weight(w4, "w4_raw", nc.sync)

        q2 = quantize(interleave(w2_raw, "w2"), "w2")
        e_codes = gather_words(e_table, seen_list[:], "e_codes")
        q1 = quantize(interleave(w1_raw, "w1"), "w1")

        def halves(name, shape, pool=sb):
            return [pool.tile(shape, F32, name="%s%d" % (name, h)) for h in range(HALVES)]

        SH = S // HALVES
        both = range(HALVES)
        x_codes = [gather_words(x_table, offs_list[:, h * SH // 16 : (h + 1) * SH // 16], "x_codes%d" % h) for h in both]
        mix_acc, val_acc = halves("mix_acc", [P, SH], ps), halves("val_acc", [P, SH], ps)
        for h in both:
            product(mix_acc[h][:], q2, e_codes[:, h * SH : (h + 1) * SH], planes[:, e_at + h * SH : e_at + (h + 1) * SH])
            product(val_acc[h][:], q1, x_codes[h][:], planes[:, x_at + h * SH : x_at + (h + 1) * SH])
        q3 = quantize(interleave(w3_raw, "w3"), "w3")
        mix = sb.tile([P, HALVES, D, VH], F32, name="mix", tag="w3_raw", align_bytes=64)
        for h in both:
            nc.scalar.activation(mix[:, h], mix_acc[h][:].rearrange("p (v d) -> p d v", d=D), ACT.Abs, scale=1.0 / D)

        kq = halves("kq", [P, D, VH])
        d_codes = gather_words(d_table, state_list[:], "d_codes")
        bias_acc = ps.tile([P, V], F32, name="bias_acc")
        product(bias_acc[:], q3, d_codes[:], planes[:, d_at : d_at + V])
        for h in both:
            nc.vector.tensor_tensor(kq[h][:], val_acc[h][:].rearrange("p (v d) -> p d v", d=D), mix[:, h], ALU.mult)

        gate_acc = halves("gate_acc", [P, VH], ps)
        w4_bf16 = interleave(w4_raw, "w4")
        mean, y, gate, ex, elu = [halves(n, [P, VH]) for n in ("mean", "y", "gate", "ex", "elu")]
        res = halves("res", [P, VH])
        low_both = sb.tile([P, HALVES, VH], F32, name="low_both", tag="w4_raw", align_bytes=64)
        low = [low_both[:, h] for h in both]
        for h in both:
            nc.vector.tensor_tensor(mean[h][:], kq[h][:, 0, :], kq[h][:, 1, :], ALU.add)
        for h in both:
            nc.vector.tensor_tensor(y[h][:], bias_acc[:, h * VH : (h + 1) * VH], mean[h][:], ALU.add)
        q4 = quantize(w4_bf16, "w4")
        for h in both:
            product(gate_acc[h][:], q4, d_codes[:, h * VH : (h + 1) * VH], planes[:, d_at + h * VH : d_at + (h + 1) * VH])
        for h in both:
            nc.vector.tensor_scalar(low[h], y[h][:], 0.0, None, ALU.min)
        for h in both:
            nc.scalar.activation(ex[h][:], low[h], ACT.Exp)
        for h in both:
            nc.scalar.activation(gate[h][:], gate_acc[h][:], ACT.Abs)
        for h in both:
            nc.vector.scalar_tensor_tensor(elu[h][:], ex[h][:], one[:], y[h][:], ALU.subtract, ALU.max)
        for h in both:
            nc.vector.tensor_tensor(res[h][:], elu[h][:], gate[h][:], ALU.mult)
            (nc.scalar, nc.sync)[h].dma_start(out[:, h * VH : (h + 1) * VH], res[h][:])
